import numpy as np, ml_dtypes
CORES = [24,26,29,31,48,50,53,55]
N = 8
TK = 512
WID = [512,192,128,128,256,512,512,64]
def setup_inputs(rng):
    return {"x": rng.standard_normal((N, 128, TK), dtype=np.float32).astype(ml_dtypes.bfloat16), "w1": (rng.standard_normal((N, 128, 128), dtype=np.float32) / 8).astype(ml_dtypes.bfloat16), "w2": (rng.standard_normal((N, 128, 128), dtype=np.float32) / 8).astype(ml_dtypes.bfloat16)}
def setup_inputs_big(rng):
    d = setup_inputs(rng)
    for k in ("x", "w1", "w2"): d[k] = (d[k].astype(np.float32) * 1024.0).astype(d[k].dtype)
    return d
def setup_inputs_small(rng):
    d = setup_inputs(rng)
    for k in ("x", "w1", "w2"): d[k] = (d[k].astype(np.float32) * (1 / 1024.0)).astype(d[k].dtype)
    return d
def setup_inputs_apart(rng):
    d = setup_inputs(rng)
    f = (10.0 ** rng.permutation(np.linspace(-1.5, 1.5, N))).astype(np.float32).reshape(N, 1, 1)
    for k in ("x", "w1", "w2"): d[k] = (d[k].astype(np.float32) * f).astype(d[k].dtype)
    return d
def whole(x, w1, w2):
    X, W1, W2 = x.astype(np.float64), w1.astype(np.float64), w2.astype(np.float64)
    y = np.zeros((N, 128, TK))
    for r in range(N):
        for j in range(N):
            y[r] += W2[j].T @ np.maximum(W1[j].T @ X[r], 0.0)
    return {"y": y.astype(ml_dtypes.bfloat16 if x.dtype != np.float64 else np.float64)}
def reference(x, w1, w2):
    o = whole(x, w1, w2)["y"].copy()
    for r in range(N):
        o[r][:, WID[r]:] = np.nan
    return {"y": o}

from concourse.bass import DstId, RemoteDMATransfer
from concourse.mybir import AluOpType

D = 128
SL = 2 * D
NR = 8
HW = 256

SCRATCH = {
    "ws": ("dram", [D, SL], "bfloat16"),
    "rh": ("dram", [D, SL], "bfloat16"),
    "rx": ("dram", [2, D, SL], "bfloat16"),
    "wsb": ("sbuf", [D, NR * SL], "bfloat16"),
    "xs": ("sbuf", [D, 512], "bfloat16"),
    "zz": ("sbuf", [D, HW], "float32"),
    "hs": ("sbuf", [D, 4 * HW], "bfloat16"),
    "ys": ("sbuf", [D, 512], "bfloat16"),
    "hp0": ("psum", [D, 512], "float32"),
    "hp1": ("psum", [D, 512], "float32"),
    "hp2": ("psum", [D, 512], "float32"),
    "hp3": ("psum", [D, 512], "float32"),
    "yp0": ("psum", [D, 512], "float32"),
    "yp1": ("psum", [D, 512], "float32"),
}
SEMAPHORES = ["stg", "xl", "zr", "p1", "p2", "rl", "cp", "st", "hop", "cx0", "cx1", "ls"] + ["a%d" % j for j in range(NR)]


def _bits(m):
    return [b for b in range(m.bit_length()) if (m >> b) & 1]


def _mask(bs):
    m = 0
    for b in bs:
        m |= 1 << b
    return m


def _plan(T, topo):
    cores = list(T.cores)
    P = {}
    for c in cores:
        near = [d for d in cores if d != c and topo.chip(d) == topo.chip(c)]
        far = [d for d in cores if topo.chip(d) != topo.chip(c)]
        on = topo.mask(c, near[0])
        for d in near:
            on &= topo.mask(c, d)
        off = topo.mask(c, far[0])
        for d in far:
            off &= topo.mask(c, d)
        P[c] = {"near": near, "far": far, "on": on, "off": off,
                "port": all(topo.may_write(c, d) for d in far)}
    for c in cores:
        p = P[c]
        if p["port"]:
            p["land"] = [d for d in p["far"] if not P[d]["port"] and topo.die(d) == topo.die(c)][0]
            p["client"] = [d for d in p["near"] if not P[d]["port"] and topo.die(d) == topo.die(c)][0]
            p["bc"] = (p["on"] & ~p["off"]) or p["on"]
        else:
            p["gate"] = [d for d in p["near"] if P[d]["port"] and topo.die(d) == topo.die(c)][0]
            p["feeder"] = [d for d in p["far"] if P[d]["port"] and topo.die(d) == topo.die(c)][0]
            p["bc"] = p["on"]
            p["hopm"] = _mask(_bits(p["on"])[:8])
    return P


def rank_program(g, core, T, topo):
    rank = T.rank_of(core)
    if rank is None:
        return
    S = T.sem
    P = _plan(T, topo)
    me = P[core]
    W = T.tables["WID"][rank]
    C = 2 if W >= 256 else 1
    w = W // C
    n1 = lambda m: len(_bits(m))

    def slot(j):
        return T.wsb[:, j * SL:(j + 1) * SL]

    def arr(j):
        return S["a%d" % j]

    g.sync.dma_start(T.ws[:, 0:D], T.w1[:, :]).then_inc(S.stg, 16)
    g.scalar.dma_start(T.ws[:, D:SL], T.w2[:, :]).then_inc(S.stg, 16)
    g.sync.dma_start(T.wsb[:, rank * SL:rank * SL + D], T.w1[:, :]).then_inc(arr(rank), 16)
    g.scalar.dma_start(T.wsb[:, rank * SL + D:(rank + 1) * SL], T.w2[:, :]).then_inc(arr(rank), 16)
    xh = W // 2
    g.sync.dma_start(T.xs[:, 0:xh], T.x[:, 0:xh]).then_inc(S.xl, 16)
    g.scalar.dma_start(T.xs[:, xh:W], T.x[:, xh:W]).then_inc(S.xl, 16)

    need = {rank: 32}
    for d in me["near"]:
        need[T.rank_of(d)] = n1(P[d]["bc"])
    early, late = [], []
    for o in me["far"]:
        if P[o]["port"]:
            mine = P[o]["land"] == core
            cnt = 16 if mine else n1(P[P[o]["land"]]["on"])
            for lst, d in ((early, o), (late, P[o]["client"])):
                need[T.rank_of(d)] = cnt
                if mine:
                    lst.insert(0, T.rank_of(d))
                else:
                    lst.append(T.rank_of(d))
    nearo = [T.rank_of(d) for d in me["near"] if not P[d]["port"]] + [T.rank_of(d) for d in me["near"] if P[d]["port"]]
    groups = [[rank], nearo, early, late]

    sent = [0]

    def write(dst, out, in_, sem, m):
        rid, pid, _ = topo.addr(dst)
        g.remote_dma(out_ap=out, in_ap=in_, remote_sem=sem, local_sem=S.ls, pid=pid, routing_id=rid, dma_engine_mask=m)
        sent[0] += n1(m)

    def fan(src, j, m):
        ids = []
        for d in me["near"]:
            rid, pid, _ = topo.addr(d)
            ids.append(DstId(rid=rid, pnc=pid))
        g.remote_dma_fused([RemoteDMATransfer(dst_ids=ids, dma_engine_mask=m, remote_sem=arr(j), srcs=[src],
                                              dsts=[slot(j) for _ in ids])], local_sem=S.ls)
        sent[0] += n1(m)

    g.wait_ge(S.stg, 32)
    if me["port"]:
        write(me["land"], T.rx[0], T.ws[:, :], S.cx0, me["off"])
        fan(T.ws[:, :], rank, me["bc"])
        g.wait_ge(S.hop, n1(P[me["client"]]["hopm"]))
        write(me["land"], T.rx[1], T.rh[:, :], S.cx1, me["off"])
    else:
        write(me["gate"], T.rh[:, :], T.ws[:, :], S.hop, me["hopm"])
        fan(T.ws[:, :], rank, me["bc"])
        f = me["feeder"]
        nx = n1(P[f]["off"])
        je, jl = T.rank_of(f), T.rank_of(P[f]["client"])
        g.sync.wait_ge(S.cx0, nx)
        g.sync.dma_start(slot(je), T.rx[0]).then_inc(arr(je), 16)
        g.scalar.wait_ge(S.cx1, nx)
        g.scalar.dma_start(slot(jl), T.rx[1]).then_inc(arr(jl), 16)
        g.wait_ge(S.cx0, nx)
        fan(T.rx[0], je, me["on"])
        g.wait_ge(S.cx1, nx)
        fan(T.rx[1], jl, me["on"])

    hp = [[T.hp0, T.hp1], [T.hp2, T.hp3]]
    yp = [T.yp0, T.yp1]

    def hsb(c, i):
        o = (2 * c + (i % 2)) * HW
        return T.hs[:, o:o + w]

    ops = []
    i = 0
    for grp in groups:
        prev = None
        for j in grp:
            ops.append((1, i, j))
            if prev is not None:
                ops.append((2,) + prev)
            prev = (i, j)
            i += 1
        ops.append((2,) + prev)

    g.tensor.wait_ge(S.xl, 32)
    for kind, i, j in ops:
        if kind == 1:
            g.tensor.wait_ge(arr(j), need[j])
            for c in range(C):
                g.tensor.matmul(hp[c][i % 2][:, 0:w], T.wsb[:, j * SL:j * SL + D], T.xs[:, c * w:(c + 1) * w],
                                True, True).then_inc(S.p1, 1)
        else:
            for c in range(C):
                g.tensor.wait_ge(S.rl, i * C + c + 1)
                g.tensor.matmul(yp[c][:, 0:w], T.wsb[:, j * SL + D:(j + 1) * SL], hsb(c, i),
                                i == 0, i == NR - 1).then_inc(S.p2, 1)

    g.vector.memset(T.zz[:, 0:w], 0.0).then_inc(S.zr, 1)
    g.vector.wait_ge(S.zr, 1)
    for i in range(NR):
        for c in range(C):
            g.vector.wait_ge(S.p1, i * C + c + 1)
            if i >= 2:
                g.vector.wait_ge(S.p2, (i - 2) * C + c + 1)
            g.vector.tensor_tensor(hsb(c, i), hp[c][i % 2][:, 0:w], T.zz[:, 0:w], AluOpType.max).then_inc(S.rl, 1)
    for c in range(C):
        g.vector.wait_ge(S.p2, (NR - 1) * C + c + 1)
        g.vector.tensor_copy(T.ys[:, c * w:(c + 1) * w], yp[c][:, 0:w]).then_inc(S.cp, 1)

    for c in range(C):
        q = g.sync if c == 0 else g.scalar
        q.wait_ge(S.cp, c + 1)
        q.dma_start(T.y[:, c * w:(c + 1) * w], T.ys[:, c * w:(c + 1) * w]).then_inc(S.st, 16)

    g.wait_ge(S.ls, sent[0])
    g.wait_ge(S.st, 16 * C)
